import numpy as np
import ml_dtypes


def mxq(x, axis, fmt="e4m3"):
    dtype, down = {"e4m3": (ml_dtypes.float8_e4m3fn, 7), "e5m2": (ml_dtypes.float8_e5m2, 14)}[fmt]
    v = np.moveaxis(np.asarray(x, np.float32).astype(ml_dtypes.bfloat16).astype(np.float64), axis, -1)
    blocks = v.reshape(v.shape[:-1] + (-1, 32))
    amax = np.abs(blocks).max(-1, keepdims=True)
    byte = np.maximum(np.where(amax > 0, np.frexp(amax)[1] - 1 + 127, 0) - down, 1)
    scale = np.exp2(byte - 127.0)
    codes = (blocks / scale).astype(np.float32).astype(dtype).astype(np.float64)
    return np.moveaxis((codes * scale).reshape(v.shape), -1, axis)


WIDE = False


def mx_kscale(k):
    if not WIDE:
        return np.ones(k)
    levels = np.array([10, -10, 5, -5, 0])
    if k % 512:
        return np.exp2(np.random.permutation(np.resize(levels, k // 32))).repeat(32)
    a = np.empty((k // 512, 16))
    for p in range(k // 512):
        a[p, :8] = np.random.permutation(np.resize(levels, 8))
        for g in range(8):
            far = levels[np.abs(levels - a[p, g]) >= 10]
            a[p, g + 8] = far[np.random.randint(len(far))]
    return np.exp2(a.ravel()).repeat(32)


def f64(x):
    return np.asarray(x).astype(np.float64)


def striped(idx):
    return np.tile(idx.reshape(-1, 16).T, (8, 1)).astype(np.uint16)


def unstriped(offs):
    return offs[:16].T.reshape(-1).astype(np.int64)


def striped8(idx):
    return np.concatenate([x.reshape(-1, 16).T for x in idx]).astype(np.uint16)


def runs(offs, k):
    lists = np.stack([offs[16 * r : 16 * r + 16].T.reshape(-1) for r in range(8)]).astype(np.int64)
    return lists[np.arange(k) % 512 // 64]


def pack_weight(w):
    k, n = w.shape
    w = f64(np.asarray(w, np.float32).astype(ml_dtypes.bfloat16)).reshape(k // 32, 32, n)
    amax = np.abs(w).max(1)
    byte = np.clip(np.where(amax > 0, np.frexp(amax)[1] - 1 + 127 - 7, 1), 1, 254)
    scaled = (w * np.exp2(127.0 - byte)[:, None, :]).reshape(k, n).astype(np.float32)
    words = np.ascontiguousarray(scaled.reshape(k // 512, 128, 4, n).transpose(0, 1, 3, 2)).astype(ml_dtypes.float8_e4m3fn).view(np.uint8)
    return words, np.ascontiguousarray(byte.astype(np.uint8).reshape(k // 512, 16, n))


def unpack_weight(words, scales):
    g, p, n, _ = words.shape
    vals = np.ascontiguousarray(words).view(ml_dtypes.float8_e4m3fn).astype(np.float64) * np.repeat(np.exp2(scales.astype(np.float64) - 127.0), 8, axis=1)[..., None]
    return vals.transpose(0, 1, 3, 2).reshape(g * 512, n)


E2M1 = np.array([0.0, 0.5, 1.0, 1.5, 2.0, 3.0, 4.0, 6.0, -0.0, -0.5, -1.0, -1.5, -2.0, -3.0, -4.0, -6.0])


def pack_fp4(w):
    k, n = w.shape
    w = f64(np.asarray(w, np.float32).astype(ml_dtypes.bfloat16)).reshape(k // 32, 32, n)
    amax = np.abs(w).max(1)
    mant, ex = np.frexp(amax / 6.0)
    byte = np.clip(np.where(amax > 0, np.where(mant > 0.5, ex, ex - 1) + 127, 1), 1, 254)
    scaled = (w * np.exp2(127.0 - byte)[:, None, :]).reshape(k, n).astype(np.float32)
    c = np.ascontiguousarray(scaled.reshape(k // 512, 128, 4, n).transpose(0, 1, 3, 2)).astype(ml_dtypes.float4_e2m1fn).view(np.uint8) & 0xF
    words = (c[..., 0::2] | (c[..., 1::2] << 4)).reshape(k // 512, 128, 2 * n)
    return np.ascontiguousarray(words), np.ascontiguousarray(byte.astype(np.uint8).reshape(k // 512, 16, n))


def unpack_fp4(words, scales):
    g, _, n = scales.shape
    words = np.ascontiguousarray(words).reshape(g, 128, n, 2)
    nib = np.empty((g, 128, n, 4), np.uint8)
    nib[..., 0::2] = words & 0xF
    nib[..., 1::2] = words >> 4
    vals = E2M1[nib] * np.repeat(np.exp2(scales.astype(np.float64) - 127.0), 8, axis=1)[..., None]
    return vals.transpose(0, 1, 3, 2).reshape(g * 512, n)


K, T, S, N, G, H, U = 512, 2048, 256, 512, 2048, 512, 512


def setup_inputs():
    n = np.random.standard_normal
    s = mx_kscale(K)[:, None]
    u = mx_kscale(K)
    packed_xT = pack_weight(n((K, T)) * s)
    packed_dT = pack_weight(n((K, G)) / s)
    packed_w1 = pack_fp4(n((H, N)) / np.sqrt(H) / u[:, None])
    perm = np.random.permutation(U)
    return {
        "x_words": packed_xT[0],
        "x_scales": packed_xT[1],
        "d_words": packed_dT[0],
        "d_scales": packed_dT[1],
        "gn": (np.random.uniform(0.5, 1.5, (H, 1)) * u[:, None]).astype(np.float32),
        "w1_words": packed_w1[0],
        "w1_scales": packed_w1[1],
        "offs": striped8(np.random.randint(0, T, (8, S))),
        "ci": striped(np.random.permutation(G)[:H]),
        "n1": striped(perm[:S]),
        "n2": striped(perm[S:]),
        "n3": striped(np.random.permutation(U)),
    }


def reference(x_words, x_scales, d_words, d_scales, gn, w1_words, w1_scales, offs, ci, n1, n2, n3):
    d_ci = unpack_weight(d_words, d_scales)[:, unstriped(ci)]
    xq = unpack_weight(x_words, x_scales)[np.arange(K)[:, None], runs(offs, K)]
    s = 0.0625 * (d_ci.T @ xq)
    z = f64(gn) * s
    h = unpack_fp4(w1_words, w1_scales).T @ mxq(z, 0, "e4m3")
    nw = 0.5 * h
    ph = np.zeros((N, U))
    ph[:, unstriped(n1)] = h
    pg = ph.copy()
    pg[:, unstriped(n2)] = nw
    return pg - pg[:, unstriped(n3)]

@@ -1,0 +1,194 @@
+from contextlib import ExitStack
+
+import concourse.mybir as mybir
+
+K, T, S, N, G, H, U = 512, 2048, 256, 512, 2048, 512, 512
+FLOPS = 2 * K * H * S + 2 * H * N * S
+
+F32 = mybir.dt.float32
+BF16 = mybir.dt.bfloat16
+I32 = mybir.dt.int32
+U32 = mybir.dt.uint32
+U16 = mybir.dt.uint16
+U8 = mybir.dt.uint8
+FP8X4 = mybir.dt.float8_e4m3fn_x4
+FP4X4 = mybir.dt.float4_e2m1fn_x4
+COPY = mybir.ActivationFunctionType.Copy
+MULT = mybir.AluOpType.mult
+SUBTRACT = mybir.AluOpType.subtract
+
+P = 128
+PACK = 4
+QUADRANT = 32
+LIST_ROWS = 16
+HALF = S // 2
+BLOCKS = N // P
+
+
+def tile_picked_hwlipagtwo_none_p_kernel(
+    tc, x_words, x_scales, d_words, d_scales, gn, w1_words, w1_scales, offs, ci, n1, n2, n3, out
+):
+    nc = tc.nc
+
+    with ExitStack() as ctx:
+        lists = ctx.enter_context(tc.tile_pool(name="lists", bufs=1))
+        keep = ctx.enter_context(tc.tile_pool(name="keep", bufs=1))
+        psum = ctx.enter_context(tc.psum_pool(name="psum", bufs=1))
+
+        def load_list(name, source):
+            tile = lists.tile(list(source.shape), U16, name=name)
+            nc.sync.dma_start(tile[:], source)
+            return tile
+
+        x_byte_table = keep.tile([P, T], U8, name="x_byte_table")
+        d_byte_table = keep.tile([P, G], U8, name="d_byte_table")
+        planes = keep.tile([P, H + S], U8, name="planes", align_bytes=64)
+        w_plane = keep.tile([P, N], U8, name="w_plane", align_bytes=64)
+        nc.gpsimd.memset(d_byte_table[:].bitcast(I32), 0)
+        nc.vector.memset(x_byte_table[:].bitcast(I32), 0)
+        nc.vector.memset(w_plane[:].bitcast(I32), 0)
+        nc.vector.memset(planes[:].bitcast(I32), 0)
+        d_plane = planes[:, :H]
+        x_plane = planes[:, H:]
+
+        d_word_table = keep.tile([P, G], U32, name="d_word_table")
+        x_word_table = keep.tile([P, T], U32, name="x_word_table")
+        offs_list = load_list("offs_list", offs)
+        ci_list = load_list("ci_list", ci)
+        nc.sync.dma_start(
+            d_word_table[:].bitcast(I32), d_words[0].rearrange("p c r -> p (c r)").bitcast(I32)
+        )
+        n1_list = load_list("n1_list", n1)
+        n2_list = load_list("n2_list", n2)
+        nc.sync.dma_start(
+            x_word_table[:].bitcast(I32), x_words[0].rearrange("p c r -> p (c r)").bitcast(I32)
+        )
+        n3_list = load_list("n3_list", n3)
+        nc.scalar.dma_start(d_byte_table[0:P:8, :].bitcast(I32), d_scales[0].bitcast(I32))
+        nc.scalar.dma_start(x_byte_table[0:P:8, :].bitcast(I32), x_scales[0].bitcast(I32))
+
+        gain = keep.tile([P, PACK], F32, name="gain")
+        nc.gpsimd.dma_start(gain[:], gn.rearrange("(p t) o -> p (t o)", t=PACK))
+        w_codes = keep.tile([P, 2 * N], U8, name="w_codes", align_bytes=64)
+        nc.gpsimd.dma_start(w_codes[:].bitcast(I32), w1_words[0].bitcast(I32))
+        for q in range(PACK):
+            nc.gpsimd.dma_start(
+                w_plane[QUADRANT * q : QUADRANT * q + PACK, :].bitcast(I32),
+                w1_scales[0, PACK * q : PACK * q + PACK, :].bitcast(I32),
+            )
+
+        pages = [keep.tile([P, U], F32, name=f"page{b}") for b in range(BLOCKS)]
+        for page in pages:
+            nc.vector.memset(page[:], 0.0)
+
+        factor = keep.tile([P, PACK], F32, name="factor")
+        nc.scalar.activation(factor[:], gain[:], COPY, scale=0.0625)
+
+        picked_bytes = keep.tile([P, H + S], U8, name="picked_bytes")
+        nc.vector.tensor_copy(
+            picked_bytes[:, :H].rearrange("p (t m) -> p m t", t=PACK),
+            d_byte_table[:].indirect(ci_list[:]),
+        )
+        nc.vector.tensor_copy(picked_bytes[:, H:], x_byte_table[:].indirect(offs_list[:]))
+        for r in range(PACK):
+            queue = nc.sync if r % 2 == 0 else nc.scalar
+            queue.dma_start(
+                planes[r:P:QUADRANT, :].bitcast(I32),
+                picked_bytes[8 * r : P : QUADRANT, :].bitcast(I32),
+            )
+
+        d_codes = keep.tile([P, H], U32, name="d_codes", align_bytes=64)
+        nc.vector.tensor_copy(
+            d_codes[:].rearrange("p (t m) -> p m t", t=PACK), d_word_table[:].indirect(ci_list[:])
+        )
+        x_codes = keep.tile([P, S], U32, name="x_codes", align_bytes=64)
+        nc.vector.tensor_copy(x_codes[:], x_word_table[:].indirect(offs_list[:]))
+
+        z_codes = keep.tile([P, S], U32, name="z_codes", align_bytes=64)
+        z_plane = keep.tile([P, S], U8, name="z_plane", align_bytes=64)
+
+        def scores(half):
+            places = slice(half * HALF, (half + 1) * HALF)
+            bank = psum.tile([P, PACK, HALF], F32, name=f"scores{half}")
+            for t in range(PACK):
+                rows = slice(t * P, (t + 1) * P)
+                nc.tensor.matmul_mx(
+                    out=bank[:, t, :],
+                    lhsT=d_codes[:, rows].bitcast(FP8X4),
+                    lhsT_scale=d_plane[:, rows],
+                    rhs=x_codes[:, places].bitcast(FP8X4),
+                    rhs_scale=x_plane[:, places],
+                    start=True,
+                    stop=True,
+                )
+            z = keep.tile([P, HALF, PACK], BF16, name=f"z{half}", align_bytes=64)
+            nc.vector.tensor_tensor(
+                z[:],
+                bank[:].rearrange("p t j -> p j t"),
+                factor[:].unsqueeze(1).to_broadcast([P, HALF, PACK]),
+                MULT,
+            )
+            nc.vector.quantize_mx(
+                out=z_codes[:, places].bitcast(FP8X4),
+                scales=z_plane[:, places],
+                in_=z[:].rearrange("p j t -> p (j t)"),
+            )
+
+        def layer(b, first, count, copy):
+            places = slice(first, first + count)
+            bank = psum.tile([P, count], F32, name=f"layer{b}_{first}")
+            nc.tensor.matmul_mx(
+                out=bank[:],
+                lhsT=w_codes[:, 2 * P * b : 2 * P * (b + 1)].bitcast(FP4X4),
+                lhsT_scale=w_plane[:, P * b : P * (b + 1)],
+                rhs=z_codes[:, places].bitcast(FP8X4),
+                rhs_scale=z_plane[:, places],
+                start=True,
+                stop=True,
+            )
+            h = keep.tile([P, count], F32, name=f"h{b}_{first}")
+            copy(h[:], bank[:])
+            return h
+
+        def scatter(b, h, slots, first, scale):
+            count = h.shape[1]
+            offsets = slots[:, first // LIST_ROWS : (first + count) // LIST_ROWS]
+            nc.scalar.activation(pages[b][:].indirect(offsets), h[:], COPY, scale=scale)
+
+        def finish(b, first, count):
+            slots = slice(first, first + count)
+            fetched = keep.tile([P, count], F32, name=f"fetched{b}_{first}")
+            offsets = n3_list[:, first // LIST_ROWS : (first + count) // LIST_ROWS]
+            nc.scalar.activation(fetched[:], pages[b][:].indirect(offsets), COPY)
+            result = keep.tile([P, count], F32, name=f"result{b}_{first}")
+            nc.vector.tensor_tensor(result[:], pages[b][:, slots], fetched[:], SUBTRACT)
+            nc.sync.dma_start(out[P * b : P * (b + 1), slots], result[:])
+
+        scores(0)
+        h00 = layer(0, 0, HALF, nc.scalar.copy)
+        h10 = layer(1, 0, HALF, nc.scalar.copy)
+        scatter(0, h00, n1_list, 0, 1.0)
+        scatter(1, h10, n1_list, 0, 1.0)
+        scatter(0, h00, n2_list, 0, 0.5)
+        scatter(1, h10, n2_list, 0, 0.5)
+        scores(1)
+        h01 = layer(0, HALF, HALF, nc.vector.tensor_copy)
+        h11 = layer(1, HALF, HALF, nc.vector.tensor_copy)
+        h2 = layer(2, 0, S, nc.vector.tensor_copy)
+        h3 = layer(3, 0, S, nc.vector.tensor_copy)
+        scatter(0, h01, n1_list, HALF, 1.0)
+        scatter(1, h11, n1_list, HALF, 1.0)
+        scatter(0, h01, n2_list, HALF, 0.5)
+        scatter(1, h11, n2_list, HALF, 0.5)
+        scatter(2, h2, n1_list, 0, 1.0)
+        finish(0, 0, U // 2)
+        finish(0, U // 2, U // 2)
+        scatter(2, h2, n2_list, 0, 0.5)
+        finish(1, 0, U // 2)
+        scatter(3, h3, n1_list, 0, 1.0)
+        finish(1, U // 2, U // 2)
+        finish(2, 0, U // 2)
+        scatter(3, h3, n2_list, 0, 0.5)
+        finish(2, U // 2, U // 2)
+        finish(3, 0, U // 2)
+        finish(3, U // 2, U // 2)

@@ -33,6 +33,7 @@ def tile_picked_hwlipagtwo_none_p_kernel(
     with ExitStack() as ctx:
         lists = ctx.enter_context(tc.tile_pool(name="lists", bufs=1))
         keep = ctx.enter_context(tc.tile_pool(name="keep", bufs=1))
+        reused = ctx.enter_context(tc.tile_pool(name="reused", bufs=1))
         psum = ctx.enter_context(tc.psum_pool(name="psum", bufs=1))
 
         def load_list(name, source):
@@ -41,11 +42,9 @@ def tile_picked_hwlipagtwo_none_p_kernel(
             return tile
 
         x_byte_table = keep.tile([P, T], U8, name="x_byte_table")
-        d_byte_table = keep.tile([P, G], U8, name="d_byte_table")
+        d_byte_table = reused.tile([P, G], U8, name="d_byte_table", offset=0, align_bytes=64)
         planes = keep.tile([P, H + S], U8, name="planes", align_bytes=64)
         w_plane = keep.tile([P, N], U8, name="w_plane", align_bytes=64)
-        nc.gpsimd.memset(d_byte_table[:].bitcast(I32), 0)
-        nc.vector.memset(x_byte_table[:].bitcast(I32), 0)
         nc.vector.memset(w_plane[:].bitcast(I32), 0)
         nc.vector.memset(planes[:].bitcast(I32), 0)
         d_plane = planes[:, :H]
@@ -53,24 +52,29 @@ def tile_picked_hwlipagtwo_none_p_kernel(
 
         d_word_table = keep.tile([P, G], U32, name="d_word_table")
         x_word_table = keep.tile([P, T], U32, name="x_word_table")
+        def load_bytes(table, scales):
+            rows = scales[0].bitcast(I32)
+            nc.sync.dma_start(
+                table[:].bitcast(I32), rows.unsqueeze(1).to_broadcast([16, 8, rows.shape[1]])
+            )
+
         offs_list = load_list("offs_list", offs)
+        load_bytes(x_byte_table, x_scales)
         ci_list = load_list("ci_list", ci)
+        load_bytes(d_byte_table, d_scales)
         nc.sync.dma_start(
             d_word_table[:].bitcast(I32), d_words[0].rearrange("p c r -> p (c r)").bitcast(I32)
         )
         n1_list = load_list("n1_list", n1)
         n2_list = load_list("n2_list", n2)
+        n3_list = load_list("n3_list", n3)
         nc.sync.dma_start(
             x_word_table[:].bitcast(I32), x_words[0].rearrange("p c r -> p (c r)").bitcast(I32)
         )
-        n3_list = load_list("n3_list", n3)
-        nc.scalar.dma_start(d_byte_table[0:P:8, :].bitcast(I32), d_scales[0].bitcast(I32))
-        nc.scalar.dma_start(x_byte_table[0:P:8, :].bitcast(I32), x_scales[0].bitcast(I32))
-
         gain = keep.tile([P, PACK], F32, name="gain")
-        nc.gpsimd.dma_start(gain[:], gn.rearrange("(p t) o -> p (t o)", t=PACK))
+        nc.sync.dma_start(gain[:], gn.rearrange("(p t) o -> p (t o)", t=PACK))
         w_codes = keep.tile([P, 2 * N], U8, name="w_codes", align_bytes=64)
-        nc.gpsimd.dma_start(w_codes[:].bitcast(I32), w1_words[0].bitcast(I32))
+        nc.sync.dma_start(w_codes[:].bitcast(I32), w1_words[0].bitcast(I32))
         for q in range(PACK):
             nc.gpsimd.dma_start(
                 w_plane[QUADRANT * q : QUADRANT * q + PACK, :].bitcast(I32),
@@ -78,30 +82,27 @@ def tile_picked_hwlipagtwo_none_p_kernel(
             )
 
         pages = [keep.tile([P, U], F32, name=f"page{b}") for b in range(BLOCKS)]
-        for page in pages:
-            nc.vector.memset(page[:], 0.0)
 
         factor = keep.tile([P, PACK], F32, name="factor")
         nc.scalar.activation(factor[:], gain[:], COPY, scale=0.0625)
 
         picked_bytes = keep.tile([P, H + S], U8, name="picked_bytes")
+        nc.vector.tensor_copy(picked_bytes[:, H:], x_byte_table[:].indirect(offs_list[:]))
         nc.vector.tensor_copy(
             picked_bytes[:, :H].rearrange("p (t m) -> p m t", t=PACK),
             d_byte_table[:].indirect(ci_list[:]),
         )
-        nc.vector.tensor_copy(picked_bytes[:, H:], x_byte_table[:].indirect(offs_list[:]))
         for r in range(PACK):
-            queue = nc.sync if r % 2 == 0 else nc.scalar
-            queue.dma_start(
+            nc.scalar.dma_start(
                 planes[r:P:QUADRANT, :].bitcast(I32),
                 picked_bytes[8 * r : P : QUADRANT, :].bitcast(I32),
             )
 
-        d_codes = keep.tile([P, H], U32, name="d_codes", align_bytes=64)
+        d_codes = reused.tile([P, H], U32, name="d_codes", offset=4 * S, align_bytes=64)
         nc.vector.tensor_copy(
             d_codes[:].rearrange("p (t m) -> p m t", t=PACK), d_word_table[:].indirect(ci_list[:])
         )
-        x_codes = keep.tile([P, S], U32, name="x_codes", align_bytes=64)
+        x_codes = reused.tile([P, S], U32, name="x_codes", offset=0, align_bytes=64)
         nc.vector.tensor_copy(x_codes[:], x_word_table[:].indirect(offs_list[:]))
 
         z_codes = keep.tile([P, S], U32, name="z_codes", align_bytes=64)
@@ -166,29 +167,24 @@ def tile_picked_hwlipagtwo_none_p_kernel(
 
         scores(0)
         h00 = layer(0, 0, HALF, nc.scalar.copy)
-        h10 = layer(1, 0, HALF, nc.scalar.copy)
         scatter(0, h00, n1_list, 0, 1.0)
-        scatter(1, h10, n1_list, 0, 1.0)
         scatter(0, h00, n2_list, 0, 0.5)
-        scatter(1, h10, n2_list, 0, 0.5)
         scores(1)
+        h1 = layer(1, 0, S, nc.vector.tensor_copy)
         h01 = layer(0, HALF, HALF, nc.vector.tensor_copy)
-        h11 = layer(1, HALF, HALF, nc.vector.tensor_copy)
         h2 = layer(2, 0, S, nc.vector.tensor_copy)
         h3 = layer(3, 0, S, nc.vector.tensor_copy)
+        scatter(1, h1, n1_list, 0, 1.0)
         scatter(0, h01, n1_list, HALF, 1.0)
-        scatter(1, h11, n1_list, HALF, 1.0)
+        scatter(1, h1, n2_list, 0, 0.5)
         scatter(0, h01, n2_list, HALF, 0.5)
-        scatter(1, h11, n2_list, HALF, 0.5)
         scatter(2, h2, n1_list, 0, 1.0)
-        finish(0, 0, U // 2)
-        finish(0, U // 2, U // 2)
-        scatter(2, h2, n2_list, 0, 0.5)
-        finish(1, 0, U // 2)
         scatter(3, h3, n1_list, 0, 1.0)
-        finish(1, U // 2, U // 2)
-        finish(2, 0, U // 2)
+        scatter(2, h2, n2_list, 0, 0.5)
         scatter(3, h3, n2_list, 0, 0.5)
-        finish(2, U // 2, U // 2)
+        for b in range(BLOCKS - 1):
+            finish(b, 0, U // 2)
+            finish(b, U // 2, U // 2)
         finish(3, 0, U // 2)
-        finish(3, U // 2, U // 2)
+        finish(3, U // 2, U // 4)
+        finish(3, 3 * U // 4, U // 4)

@@ -81,7 +81,7 @@ def tile_picked_hwlipagtwo_none_p_kernel(
                 w1_scales[0, PACK * q : PACK * q + PACK, :].bitcast(I32),
             )
 
-        pages = [keep.tile([P, U], F32, name=f"page{b}") for b in range(BLOCKS)]
+        pages = [keep.tile([P, U + LIST_ROWS], F32, name=f"page{b}") for b in range(BLOCKS)]
 
         factor = keep.tile([P, PACK], F32, name="factor")
         nc.scalar.activation(factor[:], gain[:], COPY, scale=0.0625)
@@ -135,11 +135,11 @@ def tile_picked_hwlipagtwo_none_p_kernel(
                 in_=z[:].rearrange("p j t -> p (j t)"),
             )
 
-        def layer(b, first, count, copy):
-            places = slice(first, first + count)
-            bank = psum.tile([P, count], F32, name=f"layer{b}_{first}")
+        h = keep.tile([P, BLOCKS, S], F32, name="h")
+
+        def layer(bank, b, places):
             nc.tensor.matmul_mx(
-                out=bank[:],
+                out=bank,
                 lhsT=w_codes[:, 2 * P * b : 2 * P * (b + 1)].bitcast(FP4X4),
                 lhsT_scale=w_plane[:, P * b : P * (b + 1)],
                 rhs=z_codes[:, places].bitcast(FP8X4),
@@ -147,44 +147,45 @@ def tile_picked_hwlipagtwo_none_p_kernel(
                 start=True,
                 stop=True,
             )
-            h = keep.tile([P, count], F32, name=f"h{b}_{first}")
-            copy(h[:], bank[:])
-            return h
 
-        def scatter(b, h, slots, first, scale):
-            count = h.shape[1]
-            offsets = slots[:, first // LIST_ROWS : (first + count) // LIST_ROWS]
-            nc.scalar.activation(pages[b][:].indirect(offsets), h[:], COPY, scale=scale)
+        def scatter(b, slots, places, scale):
+            offsets = slots[:, places.start // LIST_ROWS : places.stop // LIST_ROWS]
+            nc.scalar.activation(pages[b][:].indirect(offsets), h[:, b, places], COPY, scale=scale)
 
-        def finish(b, first, count):
-            slots = slice(first, first + count)
-            fetched = keep.tile([P, count], F32, name=f"fetched{b}_{first}")
-            offsets = n3_list[:, first // LIST_ROWS : (first + count) // LIST_ROWS]
+        def finish(b, slots):
+            count = slots.stop - slots.start
+            fetched = keep.tile([P, count], F32, name=f"fetched{b}_{slots.start}")
+            offsets = n3_list[:, slots.start // LIST_ROWS : slots.stop // LIST_ROWS]
             nc.scalar.activation(fetched[:], pages[b][:].indirect(offsets), COPY)
-            result = keep.tile([P, count], F32, name=f"result{b}_{first}")
+            result = keep.tile([P, count], F32, name=f"result{b}_{slots.start}")
             nc.vector.tensor_tensor(result[:], pages[b][:, slots], fetched[:], SUBTRACT)
             nc.sync.dma_start(out[P * b : P * (b + 1), slots], result[:])
 
+        first, second, both = slice(0, HALF), slice(HALF, S), slice(0, S)
+        early = range(BLOCKS - 1)
+        last = BLOCKS - 1
+
         scores(0)
-        h00 = layer(0, 0, HALF, nc.scalar.copy)
-        scatter(0, h00, n1_list, 0, 1.0)
-        scatter(0, h00, n2_list, 0, 0.5)
+        for b in early:
+            bank = psum.tile([P, HALF], F32, name=f"first{b}")
+            layer(bank[:], b, first)
+            copy = nc.scalar.copy if b == 0 else nc.vector.tensor_copy
+            copy(h[:, b, first], bank[:])
+            scatter(b, n1_list, first, 1.0)
         scores(1)
-        h1 = layer(1, 0, S, nc.vector.tensor_copy)
-        h01 = layer(0, HALF, HALF, nc.vector.tensor_copy)
-        h2 = layer(2, 0, S, nc.vector.tensor_copy)
-        h3 = layer(3, 0, S, nc.vector.tensor_copy)
-        scatter(1, h1, n1_list, 0, 1.0)
-        scatter(0, h01, n1_list, HALF, 1.0)
-        scatter(1, h1, n2_list, 0, 0.5)
-        scatter(0, h01, n2_list, HALF, 0.5)
-        scatter(2, h2, n1_list, 0, 1.0)
-        scatter(3, h3, n1_list, 0, 1.0)
-        scatter(2, h2, n2_list, 0, 0.5)
-        scatter(3, h3, n2_list, 0, 0.5)
-        for b in range(BLOCKS - 1):
-            finish(b, 0, U // 2)
-            finish(b, U // 2, U // 2)
-        finish(3, 0, U // 2)
-        finish(3, U // 2, U // 4)
-        finish(3, 3 * U // 4, U // 4)
+        bank = psum.tile([P, len(early), HALF], F32, name="second")
+        for b in early:
+            layer(bank[:, b, :], b, second)
+        nc.vector.tensor_copy(h[:, : len(early), second], bank[:])
+        bank = psum.tile([P, S], F32, name="last")
+        layer(bank[:], last, both)
+        nc.vector.tensor_copy(h[:, last, :], bank[:])
+        for b in early:
+            scatter(b, n1_list, second, 1.0)
+        scatter(last, n1_list, both, 1.0)
+        for b in range(BLOCKS):
+            scatter(b, n2_list, both, 0.5)
+        for b in early:
+            finish(b, slice(0, U))
+        finish(last, slice(0, 5 * U // 8))
+        finish(last, slice(5 * U // 8, U))

@@ -45,7 +45,7 @@ def tile_picked_hwlipagtwo_none_p_kernel(
         d_byte_table = reused.tile([P, G], U8, name="d_byte_table", offset=0, align_bytes=64)
         planes = keep.tile([P, H + S], U8, name="planes", align_bytes=64)
         w_plane = keep.tile([P, N], U8, name="w_plane", align_bytes=64)
-        nc.vector.memset(w_plane[:].bitcast(I32), 0)
+        nc.gpsimd.memset(w_plane[:].bitcast(I32), 0)
         nc.vector.memset(planes[:].bitcast(I32), 0)
         d_plane = planes[:, :H]
         x_plane = planes[:, H:]
@@ -62,12 +62,12 @@ def tile_picked_hwlipagtwo_none_p_kernel(
         load_bytes(x_byte_table, x_scales)
         ci_list = load_list("ci_list", ci)
         load_bytes(d_byte_table, d_scales)
-        nc.sync.dma_start(
-            d_word_table[:].bitcast(I32), d_words[0].rearrange("p c r -> p (c r)").bitcast(I32)
-        )
         n1_list = load_list("n1_list", n1)
         n2_list = load_list("n2_list", n2)
         n3_list = load_list("n3_list", n3)
+        nc.sync.dma_start(
+            d_word_table[:].bitcast(I32), d_words[0].rearrange("p c r -> p (c r)").bitcast(I32)
+        )
         nc.sync.dma_start(
             x_word_table[:].bitcast(I32), x_words[0].rearrange("p c r -> p (c r)").bitcast(I32)
         )
@@ -76,15 +76,13 @@ def tile_picked_hwlipagtwo_none_p_kernel(
         w_codes = keep.tile([P, 2 * N], U8, name="w_codes", align_bytes=64)
         nc.sync.dma_start(w_codes[:].bitcast(I32), w1_words[0].bitcast(I32))
         for q in range(PACK):
-            nc.gpsimd.dma_start(
+            queue = nc.sync if q == PACK - 1 else nc.gpsimd
+            queue.dma_start(
                 w_plane[QUADRANT * q : QUADRANT * q + PACK, :].bitcast(I32),
                 w1_scales[0, PACK * q : PACK * q + PACK, :].bitcast(I32),
             )
 
         pages = [keep.tile([P, U + LIST_ROWS], F32, name=f"page{b}") for b in range(BLOCKS)]
-
-        factor = keep.tile([P, PACK], F32, name="factor")
-        nc.scalar.activation(factor[:], gain[:], COPY, scale=0.0625)
 
         picked_bytes = keep.tile([P, H + S], U8, name="picked_bytes")
         nc.vector.tensor_copy(picked_bytes[:, H:], x_byte_table[:].indirect(offs_list[:]))
@@ -122,11 +120,13 @@ def tile_picked_hwlipagtwo_none_p_kernel(
                     start=True,
                     stop=True,
                 )
-            z = keep.tile([P, HALF, PACK], BF16, name=f"z{half}", align_bytes=64)
-            nc.vector.tensor_tensor(
+            z = keep.tile([P, HALF, PACK], BF16, name="z", align_bytes=64)
+            nc.vector.scalar_tensor_tensor(
                 z[:],
                 bank[:].rearrange("p t j -> p j t"),
-                factor[:].unsqueeze(1).to_broadcast([P, HALF, PACK]),
+                0.0625,
+                gain[:].unsqueeze(1).to_broadcast([P, HALF, PACK]),
+                MULT,
                 MULT,
             )
             nc.vector.quantize_mx(

from contextlib import ExitStack

import concourse.mybir as mybir

K, T, S, N, G, H, U = 512, 2048, 256, 512, 2048, 512, 512
FLOPS = 2 * K * H * S + 2 * H * N * S

F32 = mybir.dt.float32
BF16 = mybir.dt.bfloat16
I32 = mybir.dt.int32
U32 = mybir.dt.uint32
U16 = mybir.dt.uint16
U8 = mybir.dt.uint8
FP8X4 = mybir.dt.float8_e4m3fn_x4
FP4X4 = mybir.dt.float4_e2m1fn_x4
COPY = mybir.ActivationFunctionType.Copy
MULT = mybir.AluOpType.mult
SUBTRACT = mybir.AluOpType.subtract

P = 128
PACK = 4
QUADRANT = 32
LIST_ROWS = 16
HALF = S // 2
BLOCKS = N // P


def tile_picked_hwlipagtwo_none_p_kernel(
    tc, x_words, x_scales, d_words, d_scales, gn, w1_words, w1_scales, offs, ci, n1, n2, n3, out
):
    nc = tc.nc

    with ExitStack() as ctx:
        lists = ctx.enter_context(tc.tile_pool(name="lists", bufs=1))
        keep = ctx.enter_context(tc.tile_pool(name="keep", bufs=1))
        reused = ctx.enter_context(tc.tile_pool(name="reused", bufs=1))
        psum = ctx.enter_context(tc.psum_pool(name="psum", bufs=1))

        def load_list(name, source):
            tile = lists.tile(list(source.shape), U16, name=name)
            nc.sync.dma_start(tile[:], source)
            return tile

        x_byte_table = keep.tile([P, T], U8, name="x_byte_table")
        d_byte_table = reused.tile([P, G], U8, name="d_byte_table", offset=0, align_bytes=64)
        planes = keep.tile([P, H + S], U8, name="planes", align_bytes=64)
        w_plane = keep.tile([P, N], U8, name="w_plane", align_bytes=64)
        nc.gpsimd.memset(w_plane[:].bitcast(I32), 0)
        nc.vector.memset(planes[:].bitcast(I32), 0)
        d_plane = planes[:, :H]
        x_plane = planes[:, H:]

        d_word_table = keep.tile([P, G], U32, name="d_word_table")
        x_word_table = keep.tile([P, T], U32, name="x_word_table")
        def load_bytes(table, scales):
            rows = scales[0].bitcast(I32)
            nc.sync.dma_start(
                table[:].bitcast(I32), rows.unsqueeze(1).to_broadcast([16, 8, rows.shape[1]])
            )

        offs_list = load_list("offs_list", offs)
        load_bytes(x_byte_table, x_scales)
        ci_list = load_list("ci_list", ci)
        load_bytes(d_byte_table, d_scales)
        n1_list = load_list("n1_list", n1)
        n2_list = load_list("n2_list", n2)
        n3_list = load_list("n3_list", n3)
        nc.sync.dma_start(
            d_word_table[:].bitcast(I32), d_words[0].rearrange("p c r -> p (c r)").bitcast(I32)
        )
        nc.sync.dma_start(
            x_word_table[:].bitcast(I32), x_words[0].rearrange("p c r -> p (c r)").bitcast(I32)
        )
        gain = keep.tile([P, PACK], F32, name="gain")
        nc.sync.dma_start(gain[:], gn.rearrange("(p t) o -> p (t o)", t=PACK))
        w_codes = keep.tile([P, 2 * N], U8, name="w_codes", align_bytes=64)
        nc.sync.dma_start(w_codes[:].bitcast(I32), w1_words[0].bitcast(I32))
        for q in range(PACK):
            queue = nc.sync if q == PACK - 1 else nc.gpsimd
            queue.dma_start(
                w_plane[QUADRANT * q : QUADRANT * q + PACK, :].bitcast(I32),
                w1_scales[0, PACK * q : PACK * q + PACK, :].bitcast(I32),
            )

        pages = [keep.tile([P, U + LIST_ROWS], F32, name=f"page{b}") for b in range(BLOCKS)]

        picked_bytes = keep.tile([P, H + S], U8, name="picked_bytes")
        nc.vector.tensor_copy(picked_bytes[:, H:], x_byte_table[:].indirect(offs_list[:]))
        nc.vector.tensor_copy(
            picked_bytes[:, :H].rearrange("p (t m) -> p m t", t=PACK),
            d_byte_table[:].indirect(ci_list[:]),
        )
        for r in range(PACK):
            nc.scalar.dma_start(
                planes[r:P:QUADRANT, :].bitcast(I32),
                picked_bytes[8 * r : P : QUADRANT, :].bitcast(I32),
            )

        d_codes = reused.tile([P, H], U32, name="d_codes", offset=4 * S, align_bytes=64)
        nc.vector.tensor_copy(
            d_codes[:].rearrange("p (t m) -> p m t", t=PACK), d_word_table[:].indirect(ci_list[:])
        )
        x_codes = reused.tile([P, S], U32, name="x_codes", offset=0, align_bytes=64)
        nc.vector.tensor_copy(x_codes[:], x_word_table[:].indirect(offs_list[:]))

        z_codes = keep.tile([P, S], U32, name="z_codes", align_bytes=64)
        z_plane = keep.tile([P, S], U8, name="z_plane", align_bytes=64)

        def scores(half):
            places = slice(half * HALF, (half + 1) * HALF)
            bank = psum.tile([P, PACK, HALF], F32, name=f"scores{half}")
            for t in range(PACK):
                rows = slice(t * P, (t + 1) * P)
                nc.tensor.matmul_mx(
                    out=bank[:, t, :],
                    lhsT=d_codes[:, rows].bitcast(FP8X4),
                    lhsT_scale=d_plane[:, rows],
                    rhs=x_codes[:, places].bitcast(FP8X4),
                    rhs_scale=x_plane[:, places],
                    start=True,
                    stop=True,
                )
            z = keep.tile([P, HALF, PACK], BF16, name="z", align_bytes=64)
            nc.vector.scalar_tensor_tensor(
                z[:],
                bank[:].rearrange("p t j -> p j t"),
                0.0625,
                gain[:].unsqueeze(1).to_broadcast([P, HALF, PACK]),
                MULT,
                MULT,
            )
            nc.vector.quantize_mx(
                out=z_codes[:, places].bitcast(FP8X4),
                scales=z_plane[:, places],
                in_=z[:].rearrange("p j t -> p (j t)"),
            )

        h = keep.tile([P, BLOCKS, S], F32, name="h")

        def layer(bank, b, places):
            nc.tensor.matmul_mx(
                out=bank,
                lhsT=w_codes[:, 2 * P * b : 2 * P * (b + 1)].bitcast(FP4X4),
                lhsT_scale=w_plane[:, P * b : P * (b + 1)],
                rhs=z_codes[:, places].bitcast(FP8X4),
                rhs_scale=z_plane[:, places],
                start=True,
                stop=True,
            )

        def scatter(b, slots, places, scale):
            offsets = slots[:, places.start // LIST_ROWS : places.stop // LIST_ROWS]
            nc.scalar.activation(pages[b][:].indirect(offsets), h[:, b, places], COPY, scale=scale)

        def finish(b, slots):
            count = slots.stop - slots.start
            fetched = keep.tile([P, count], F32, name=f"fetched{b}_{slots.start}")
            offsets = n3_list[:, slots.start // LIST_ROWS : slots.stop // LIST_ROWS]
            nc.scalar.activation(fetched[:], pages[b][:].indirect(offsets), COPY)
            result = keep.tile([P, count], F32, name=f"result{b}_{slots.start}")
            nc.vector.tensor_tensor(result[:], pages[b][:, slots], fetched[:], SUBTRACT)
            nc.sync.dma_start(out[P * b : P * (b + 1), slots], result[:])

        first, second, both = slice(0, HALF), slice(HALF, S), slice(0, S)
        early = range(BLOCKS - 1)
        last = BLOCKS - 1

        scores(0)
        for b in early:
            bank = psum.tile([P, HALF], F32, name=f"first{b}")
            layer(bank[:], b, first)
            copy = nc.scalar.copy if b == 0 else nc.vector.tensor_copy
            copy(h[:, b, first], bank[:])
            scatter(b, n1_list, first, 1.0)
        scores(1)
        bank = psum.tile([P, len(early), HALF], F32, name="second")
        for b in early:
            layer(bank[:, b, :], b, second)
        nc.vector.tensor_copy(h[:, : len(early), second], bank[:])
        bank = psum.tile([P, S], F32, name="last")
        layer(bank[:], last, both)
        nc.vector.tensor_copy(h[:, last, :], bank[:])
        for b in early:
            scatter(b, n1_list, second, 1.0)
        scatter(last, n1_list, both, 1.0)
        for b in range(BLOCKS):
            scatter(b, n2_list, both, 0.5)
        for b in early:
            finish(b, slice(0, U))
        finish(last, slice(0, 5 * U // 8))
        finish(last, slice(5 * U // 8, U))
